import numpy as np
import ml_dtypes


def mxq(x, axis, fmt="e4m3"):
    dtype, down = {"e4m3": (ml_dtypes.float8_e4m3fn, 7), "e5m2": (ml_dtypes.float8_e5m2, 14)}[fmt]
    v = np.moveaxis(np.asarray(x, np.float32).astype(ml_dtypes.bfloat16).astype(np.float64), axis, -1)
    blocks = v.reshape(v.shape[:-1] + (-1, 32))
    amax = np.abs(blocks).max(-1, keepdims=True)
    byte = np.maximum(np.where(amax > 0, np.frexp(amax)[1] - 1 + 127, 0) - down, 1)
    scale = np.exp2(byte - 127.0)
    codes = (blocks / scale).astype(np.float32).astype(dtype).astype(np.float64)
    return np.moveaxis((codes * scale).reshape(v.shape), -1, axis)


WIDE = False


def mx_kscale(k):
    if not WIDE:
        return np.ones(k)
    levels = np.array([10, -10, 5, -5, 0])
    if k % 512:
        return np.exp2(np.random.permutation(np.resize(levels, k // 32))).repeat(32)
    a = np.empty((k // 512, 16))
    for p in range(k // 512):
        a[p, :8] = np.random.permutation(np.resize(levels, 8))
        for g in range(8):
            far = levels[np.abs(levels - a[p, g]) >= 10]
            a[p, g + 8] = far[np.random.randint(len(far))]
    return np.exp2(a.ravel()).repeat(32)


def f64(x):
    return np.asarray(x).astype(np.float64)


def striped(idx):
    return np.tile(idx.reshape(-1, 16).T, (8, 1)).astype(np.uint16)


def unstriped(offs):
    return offs[:16].T.reshape(-1).astype(np.int64)


def pack_weight(w):
    k, n = w.shape
    w = f64(np.asarray(w, np.float32).astype(ml_dtypes.bfloat16)).reshape(k // 32, 32, n)
    amax = np.abs(w).max(1)
    byte = np.clip(np.where(amax > 0, np.frexp(amax)[1] - 1 + 127 - 7, 1), 1, 254)
    scaled = (w * np.exp2(127.0 - byte)[:, None, :]).reshape(k, n).astype(np.float32)
    words = np.ascontiguousarray(scaled.reshape(k // 512, 128, 4, n).transpose(0, 1, 3, 2)).astype(ml_dtypes.float8_e4m3fn).view(np.uint8)
    return words, np.ascontiguousarray(byte.astype(np.uint8).reshape(k // 512, 16, n))


def unpack_weight(words, scales):
    g, p, n, _ = words.shape
    vals = np.ascontiguousarray(words).view(ml_dtypes.float8_e4m3fn).astype(np.float64) * np.repeat(np.exp2(scales.astype(np.float64) - 127.0), 8, axis=1)[..., None]
    return vals.transpose(0, 1, 3, 2).reshape(g * 512, n)


K, T, S, H, Z, W = 512, 2048, 512, 512, 512, 1024
P = 2 ** 7


def setup_inputs():
    n = np.random.standard_normal
    s = mx_kscale(K)[:, None]
    u = mx_kscale(H)
    packed_xT = pack_weight(n((K, T)) * s)
    packed_eT = pack_weight(n((K, W)) * s)
    return {
        "x_words": packed_xT[0],
        "x_scales": packed_xT[1],
        "w1": (n((K, H)) / np.sqrt(K) / s).astype(np.float32),
        "w2": (n((K, H)) / np.sqrt(K) / s).astype(np.float32),
        "e_words": packed_eT[0],
        "e_scales": packed_eT[1],
        "w3": (n((K, H)) / np.sqrt(K) / s).astype(np.float32),
        "unit": (np.random.uniform(0.6, 1.4, (H, 1)) * u[:, None]).astype(np.float32),
        "unit2": (np.random.uniform(0.6, 1.4, (H, 1)) / np.sqrt(H) / u[:, None]).astype(np.float32),
        "noi": (np.tile(np.random.uniform(0.3, 1.0, W), (P, 1))).astype(np.float32),
        "offs": striped(np.random.permutation(T)[:S]),
        "txb": striped(np.random.permutation(W)[:Z]),
        "pol": striped(np.random.permutation(S)),
        "adj": striped(np.random.permutation(Z)),
    }


def reference(x_words, x_scales, w1, w2, e_words, e_scales, w3, unit, unit2, noi, offs, txb, pol, adj):
    xq = unpack_weight(x_words, x_scales)[:, unstriped(offs)]
    re = mxq(f64(w1), 0, "e4m3").T @ xq
    im2 = mxq(f64(w2), 0, "e4m3").T @ xq
    ip = im2[:, unstriped(pol)]
    rx = re * np.tanh(ip) + 0.4 * re
    hid = f64(unit) * rx
    e_txb = unpack_weight(e_words, e_scales)[:, unstriped(txb)]
    ye = mxq(f64(w3), 0, "e4m3").T @ e_txb
    hid2 = f64(unit2) * ye
    sc = mxq(hid, 0, "e4m3").T @ mxq(hid2, 0, "e4m3")
    pow_ = (sc) ** 2
    itf = 0.5 * pow_[:, unstriped(adj)]
    sinr = pow_ / (itf + f64(noi)[:1][:, unstriped(txb)] + 0.2)
    return np.log(sinr + 1.0)

@@ -1,0 +1,206 @@
+from contextlib import ExitStack
+
+import concourse.mybir as mybir
+
+F32 = mybir.dt.float32
+BF16 = mybir.dt.bfloat16
+I32 = mybir.dt.int32
+U32 = mybir.dt.uint32
+U16 = mybir.dt.uint16
+U8 = mybir.dt.uint8
+FP8X4 = mybir.dt.float8_e4m3fn_x4
+ALU = mybir.AluOpType
+ACT = mybir.ActivationFunctionType
+
+P = 128
+PACK = 4
+S = 512
+HALF = S // 2
+FLOPS = 4 * 2 * 512 * 512 * 512
+
+
+def tile_picked_ybeamsl_rate_p_kernel(
+    tc, x_words, x_scales, w1, w2, e_words, e_scales, w3, unit, unit2, noi, offs, txb, pol, adj, out
+):
+    nc = tc.nc
+    with ExitStack() as ctx:
+        keep = ctx.enter_context(tc.tile_pool(name="keep", bufs=1))
+        psum = ctx.enter_context(tc.psum_pool(name="psum", bufs=8))
+
+        def sbuf(name, shape, dtype):
+            return keep.tile(shape, dtype, name=name, align_bytes=64)
+
+        def bank(shape):
+            return psum.tile(shape, F32, name="bank")
+
+        def load_list(name, src):
+            lst = sbuf(name, [P, S // 16], U16)
+            nc.sync.dma_start(lst[:], src)
+            return lst
+
+        def load_words(name, src):
+            table = sbuf(name, [P, src.shape[2]], U32)
+            nc.sync.dma_start(table[:].bitcast(I32), src[0].rearrange("p n t -> p (n t)").bitcast(I32))
+            return table
+
+        def scale_table(name, src):
+            table = sbuf(name, [P, src.shape[2]], U8)
+            nc.vector.memset(table[:].bitcast(I32), 0)
+            return table
+
+        def load_scales(table, src):
+            for q in range(4):
+                nc.sync.dma_start(
+                    table[32 * q : 32 * q + 4, :].bitcast(I32), src[0, 4 * q : 4 * q + 4, :].bitcast(I32)
+                )
+
+        def load_weight(name, src, h):
+            raw = sbuf("%s_raw%d" % (name, h), [P, PACK, HALF], F32)
+            nc.sync.dma_start(raw[:], src[:, h * HALF : (h + 1) * HALF].rearrange("(p j) c -> p j c", j=PACK))
+            return raw
+
+        def load_factor(name, src):
+            fac = sbuf(name, [P, PACK], F32)
+            nc.sync.dma_start(fac[:], src.rearrange("(p t) o -> p (t o)", t=PACK))
+            return fac
+
+        def gather(name, table, lst, dtype):
+            picked = sbuf(name, [P, S], dtype)
+            nc.vector.tensor_copy(picked[:], table[:].indirect(lst[:]))
+            return picked
+
+        def round_weight(name, raws, copy):
+            grouped = sbuf(name + "_bf16", [P, PACK * S], BF16)
+            view = grouped[:].rearrange("p (t m j) -> p m j t", t=PACK, j=PACK)
+            step = P // len(raws)
+            for h, raw in enumerate(raws):
+                copy(view[:, h * step : (h + 1) * step], raw[:].rearrange("p j (m t) -> p m j t", t=PACK))
+            return grouped
+
+        def quantize(name, grouped, width):
+            codes = sbuf(name + "_codes", [P, width], U32)
+            scales = sbuf(name + "_scales", [P, width], U8)
+            nc.vector.quantize_mx(out=codes[:].bitcast(FP8X4), scales=scales[:], in_=grouped)
+            return codes, scales
+
+        def product(acc, stationary, m0, moving, n0, n):
+            nc.tensor.matmul_mx(
+                out=acc,
+                lhsT=stationary[0][:, m0 : m0 + P].bitcast(FP8X4),
+                lhsT_scale=stationary[1][:, m0 : m0 + P],
+                rhs=moving[0][:, n0 : n0 + n].bitcast(FP8X4),
+                rhs_scale=moving[1][:, n0 : n0 + n],
+                start=True,
+                stop=True,
+            )
+
+        xs_table = scale_table("xs_table", x_scales)
+        es_table = scale_table("es_table", e_scales)
+        offs_l = load_list("offs_l", offs)
+        w2_raw = [load_weight("w2", w2, 0)]
+        load_scales(xs_table, x_scales)
+        w2_raw.append(load_weight("w2", w2, 1))
+        txb_l = load_list("txb_l", txb)
+        load_scales(es_table, e_scales)
+        xw_table = load_words("xw_table", x_words)
+        ew_table = load_words("ew_table", e_words)
+        w3_raw = [load_weight("w3", w3, h) for h in range(2)]
+        u2 = load_factor("u2", unit2)
+        w1_raw = [load_weight("w1", w1, h) for h in range(2)]
+        pol_l = load_list("pol_l", pol)
+        u1 = load_factor("u1", unit)
+        noi_sb = sbuf("noi_sb", [P, noi.shape[1]], F32)
+        nc.sync.dma_start(noi_sb[:], noi)
+        adj_l = load_list("adj_l", adj)
+
+        xs = gather("xs", xs_table, offs_l, U8)
+        w2_bf = round_weight("w2", w2_raw, nc.scalar.copy)
+        es = gather("es", es_table, txb_l, U8)
+        w2q = quantize("w2", w2_bf[:], S)
+        xw = gather("xw", xw_table, offs_l, U32)
+        xq = (xw, xs)
+
+        tanh_im = []
+        for t in range(PACK):
+            acc = bank([P, S])
+            product(acc[:], w2q, P * t, xq, 0, S)
+            th = sbuf("tanh%d" % t, [P, S], F32)
+            nc.scalar.activation(th[:], acc[:], ACT.Tanh)
+            tanh_im.append(th)
+
+        ew = gather("ew", ew_table, txb_l, U32)
+        eq = (ew, es)
+
+        def partner(h, planes):
+            for t in range(PACK):
+                nc.scalar.activation(
+                    planes[:, t, :], tanh_im[t][:].indirect(pol_l[:, 16 * h : 16 * (h + 1)]), ACT.Copy, bias=0.4
+                )
+            return planes
+
+        w3q = quantize("w3", round_weight("w3", w3_raw, nc.vector.tensor_copy)[:], S)
+        hid2_bf = sbuf("hid2_bf16", [P, S, PACK], BF16)
+        for b in range(S // P):
+            acc = bank([P, PACK, P])
+            for t in range(PACK):
+                product(acc[:, t, :], w3q, P * t, eq, P * b, P)
+            nc.vector.tensor_tensor(
+                hid2_bf[:, P * b : P * (b + 1), :],
+                acc[:].rearrange("p t n -> p n t"),
+                u2[:].unsqueeze(1).to_broadcast([P, P, PACK]),
+                ALU.mult,
+            )
+        w1_bf = round_weight("w1", w1_raw, nc.scalar.copy)
+        mod = [partner(0, w1_raw[1])]
+        hid2q = quantize("hid2", hid2_bf[:].rearrange("p n t -> p (n t)"), S)
+        w1q = quantize("w1", w1_bf[:], S)
+        mod.append(partner(1, w1_bf[:].bitcast(F32).rearrange("p (t n) -> p t n", t=PACK)))
+
+        floor = sbuf("floor", [P, S], F32)
+        nc.scalar.activation(floor[:], noi_sb[:].indirect(txb_l[:]), ACT.Copy, bias=0.4, scale=2.0)
+
+        re = []
+        for t in range(PACK):
+            acc = bank([P, S])
+            product(acc[:], w1q, P * t, xq, 0, S)
+            re.append(acc)
+
+        hidq = []
+        for h in range(2):
+            planes = sbuf("hid_planes%d" % h, [P, PACK, HALF], BF16)
+            for t in range(PACK):
+                nc.vector.scalar_tensor_tensor(
+                    planes[:, t, :],
+                    re[t][:, HALF * h : HALF * (h + 1)],
+                    u1[:, t : t + 1],
+                    mod[h][:, t, :],
+                    ALU.mult,
+                    ALU.mult,
+                )
+            hid_bf = sbuf("hid_bf16_%d" % h, [P, HALF, PACK], BF16)
+            nc.vector.tensor_copy(
+                hid_bf[:].rearrange("p (c i) t -> p c t i", i=4),
+                planes[:].rearrange("p t (c i) -> p c t i", i=4),
+            )
+            hidq.append(quantize("hid%d" % h, hid_bf[:].rearrange("p n t -> p (n t)"), HALF))
+
+        for a in range(S // P):
+            acc = bank([P, S])
+            product(acc[:], hidq[a // 2], P * (a % 2), hid2q, 0, S)
+            power = sbuf("power%d" % a, [P, S], F32)
+            nc.scalar.activation(power[:], acc[:], ACT.Square)
+            den = sbuf("den%d" % a, [P, S], F32)
+            for h in range(2):
+                cols = slice(HALF * h, HALF * (h + 1))
+                nc.vector.tensor_tensor(
+                    den[:, cols], power[:].indirect(adj_l[:, 16 * h : 16 * (h + 1)]), floor[:, cols], ALU.add
+                )
+            num = sbuf("num%d" % a, [P, S], F32)
+            nc.vector.scalar_tensor_tensor(num[:], power[:], 2.0, den[:], ALU.mult, ALU.add)
+            ln_den = sbuf("ln_den%d" % a, [P, S], F32)
+            nc.scalar.activation(ln_den[:], den[:], ACT.Ln)
+            ln_num = sbuf("ln_num%d" % a, [P, S], F32)
+            nc.scalar.activation(ln_num[:], num[:], ACT.Ln)
+            rate = sbuf("rate%d" % a, [P, S], F32)
+            nc.vector.tensor_tensor(rate[:], ln_num[:], ln_den[:], ALU.subtract)
+            nc.sync.dma_start(out[P * a : P * (a + 1), :], rate[:])

@@ -106,8 +106,8 @@ def tile_picked_ybeamsl_rate_p_kernel(
         ew_table = load_words("ew_table", e_words)
         w3_raw = [load_weight("w3", w3, h) for h in range(2)]
         u2 = load_factor("u2", unit2)
-        w1_raw = [load_weight("w1", w1, h) for h in range(2)]
         pol_l = load_list("pol_l", pol)
+        w1_raw = [load_weight("w1", w1, h) for h in range(2)]
         u1 = load_factor("u1", unit)
         noi_sb = sbuf("noi_sb", [P, noi.shape[1]], F32)
         nc.sync.dma_start(noi_sb[:], noi)
@@ -131,14 +131,17 @@ def tile_picked_ybeamsl_rate_p_kernel(
         ew = gather("ew", ew_table, txb_l, U32)
         eq = (ew, es)
 
-        def partner(h, planes):
+        mod = []
+        for h in range(2):
+            picked = sbuf("mod%d" % h, [P, PACK, HALF], F32)
             for t in range(PACK):
                 nc.scalar.activation(
-                    planes[:, t, :], tanh_im[t][:].indirect(pol_l[:, 16 * h : 16 * (h + 1)]), ACT.Copy, bias=0.4
+                    picked[:, t, :], tanh_im[t][:].indirect(pol_l[:, 16 * h : 16 * (h + 1)]), ACT.Copy, bias=0.4
                 )
-            return planes
+            mod.append(picked)
 
         w3q = quantize("w3", round_weight("w3", w3_raw, nc.vector.tensor_copy)[:], S)
+        w1q = quantize("w1", round_weight("w1", w1_raw, nc.vector.tensor_copy)[:], S)
         hid2_bf = sbuf("hid2_bf16", [P, S, PACK], BF16)
         for b in range(S // P):
             acc = bank([P, PACK, P])
@@ -150,20 +153,19 @@ def tile_picked_ybeamsl_rate_p_kernel(
                 u2[:].unsqueeze(1).to_broadcast([P, P, PACK]),
                 ALU.mult,
             )
-        w1_bf = round_weight("w1", w1_raw, nc.scalar.copy)
-        mod = [partner(0, w1_raw[1])]
         hid2q = quantize("hid2", hid2_bf[:].rearrange("p n t -> p (n t)"), S)
-        w1q = quantize("w1", w1_bf[:], S)
-        mod.append(partner(1, w1_bf[:].bitcast(F32).rearrange("p (t n) -> p t n", t=PACK)))
 
         floor = sbuf("floor", [P, S], F32)
         nc.scalar.activation(floor[:], noi_sb[:].indirect(txb_l[:]), ACT.Copy, bias=0.4, scale=2.0)
 
-        re = []
-        for t in range(PACK):
-            acc = bank([P, S])
-            product(acc[:], w1q, P * t, xq, 0, S)
-            re.append(acc)
+        re = {}
+        for h in range(2):
+            for pair in range(PACK // 2):
+                acc = bank([P, 2, HALF])
+                for i in range(2):
+                    t = 2 * pair + i
+                    product(acc[:, i, :], w1q, P * t, xq, HALF * h, HALF)
+                    re[h, t] = acc[:, i, :]
 
         hidq = []
         for h in range(2):
@@ -171,32 +173,37 @@ def tile_picked_ybeamsl_rate_p_kernel(
             for t in range(PACK):
                 nc.vector.scalar_tensor_tensor(
                     planes[:, t, :],
-                    re[t][:, HALF * h : HALF * (h + 1)],
+                    re[h, t],
                     u1[:, t : t + 1],
                     mod[h][:, t, :],
                     ALU.mult,
                     ALU.mult,
                 )
             hid_bf = sbuf("hid_bf16_%d" % h, [P, HALF, PACK], BF16)
-            nc.vector.tensor_copy(
+            (nc.scalar.copy, nc.vector.tensor_copy)[h](
                 hid_bf[:].rearrange("p (c i) t -> p c t i", i=4),
                 planes[:].rearrange("p t (c i) -> p c t i", i=4),
             )
             hidq.append(quantize("hid%d" % h, hid_bf[:].rearrange("p n t -> p (n t)"), HALF))
 
+        windows = []
         for a in range(S // P):
             acc = bank([P, S])
             product(acc[:], hidq[a // 2], P * (a % 2), hid2q, 0, S)
-            power = sbuf("power%d" % a, [P, S], F32)
-            nc.scalar.activation(power[:], acc[:], ACT.Square)
+            window = sbuf("power%d" % a, [P, S + 32], F32)
+            nc.scalar.activation(window[:, :S], acc[:], ACT.Square)
+            windows.append(window)
+
+        for a, window in enumerate(windows):
             den = sbuf("den%d" % a, [P, S], F32)
-            for h in range(2):
-                cols = slice(HALF * h, HALF * (h + 1))
-                nc.vector.tensor_tensor(
-                    den[:, cols], power[:].indirect(adj_l[:, 16 * h : 16 * (h + 1)]), floor[:, cols], ALU.add
-                )
+            if a == 1:
+                leak = sbuf("leak", [P, S], F32)
+                nc.scalar.activation(leak[:], window[:].indirect(adj_l[:]), ACT.Copy)
+                nc.vector.tensor_tensor(den[:], leak[:], floor[:], ALU.add)
+            else:
+                nc.vector.tensor_tensor(den[:], window[:].indirect(adj_l[:]), floor[:], ALU.add)
             num = sbuf("num%d" % a, [P, S], F32)
-            nc.vector.scalar_tensor_tensor(num[:], power[:], 2.0, den[:], ALU.mult, ALU.add)
+            nc.vector.scalar_tensor_tensor(num[:], window[:, :S], 2.0, den[:], ALU.mult, ALU.add)
             ln_den = sbuf("ln_den%d" % a, [P, S], F32)
             nc.scalar.activation(ln_den[:], den[:], ACT.Ln)
             ln_num = sbuf("ln_num%d" % a, [P, S], F32)

@@ -1,6 +1,7 @@
 from contextlib import ExitStack
 
 import concourse.mybir as mybir
+from concourse.masks import make_identity
 
 F32 = mybir.dt.float32
 BF16 = mybir.dt.bfloat16
@@ -16,7 +17,13 @@ P = 128
 PACK = 4
 S = 512
 HALF = S // 2
-FLOPS = 4 * 2 * 512 * 512 * 512
+GROUP = 16
+QUADRANT = 32
+LINE = 4
+BANKS = 8
+SPARE = 32
+TURNED_TILES = 2
+FLOPS = 4 * 2 * S * S * S
 
 
 def tile_picked_ybeamsl_rate_p_kernel(
@@ -25,7 +32,7 @@ def tile_picked_ybeamsl_rate_p_kernel(
     nc = tc.nc
     with ExitStack() as ctx:
         keep = ctx.enter_context(tc.tile_pool(name="keep", bufs=1))
-        psum = ctx.enter_context(tc.psum_pool(name="psum", bufs=8))
+        psum = ctx.enter_context(tc.psum_pool(name="psum", bufs=BANKS))
 
         def sbuf(name, shape, dtype):
             return keep.tile(shape, dtype, name=name, align_bytes=64)
@@ -34,53 +41,54 @@ def tile_picked_ybeamsl_rate_p_kernel(
             return psum.tile(shape, F32, name="bank")
 
         def load_list(name, src):
-            lst = sbuf(name, [P, S // 16], U16)
-            nc.sync.dma_start(lst[:], src)
-            return lst
+            entries = sbuf(name, [P, S // GROUP], U16)
+            nc.sync.dma_start(entries[:], src)
+            return entries
 
         def load_words(name, src):
             table = sbuf(name, [P, src.shape[2]], U32)
-            nc.sync.dma_start(table[:].bitcast(I32), src[0].rearrange("p n t -> p (n t)").bitcast(I32))
+            nc.sync.dma_start(table[:].bitcast(I32), src[0].rearrange("p n j -> p (n j)").bitcast(I32))
             return table
 
-        def scale_table(name, src):
+        def cleared_scale_table(name, src):
             table = sbuf(name, [P, src.shape[2]], U8)
             nc.vector.memset(table[:].bitcast(I32), 0)
             return table
 
         def load_scales(table, src):
-            for q in range(4):
+            for q in range(P // QUADRANT):
                 nc.sync.dma_start(
-                    table[32 * q : 32 * q + 4, :].bitcast(I32), src[0, 4 * q : 4 * q + 4, :].bitcast(I32)
+                    table[QUADRANT * q : QUADRANT * q + 4, :].bitcast(I32),
+                    src[0, 4 * q : 4 * q + 4, :].bitcast(I32),
                 )
 
-        def load_weight(name, src, h):
+        def load_weight_half(name, src, h):
             raw = sbuf("%s_raw%d" % (name, h), [P, PACK, HALF], F32)
             nc.sync.dma_start(raw[:], src[:, h * HALF : (h + 1) * HALF].rearrange("(p j) c -> p j c", j=PACK))
             return raw
 
         def load_factor(name, src):
-            fac = sbuf(name, [P, PACK], F32)
-            nc.sync.dma_start(fac[:], src.rearrange("(p t) o -> p (t o)", t=PACK))
-            return fac
+            factor = sbuf(name, [P, PACK], F32)
+            nc.gpsimd.dma_start(factor[:], src.rearrange("(p t) o -> p (t o)", t=PACK))
+            return factor
 
-        def gather(name, table, lst, dtype):
+        def gather(name, table, entries, dtype):
             picked = sbuf(name, [P, S], dtype)
-            nc.vector.tensor_copy(picked[:], table[:].indirect(lst[:]))
+            nc.vector.tensor_copy(picked[:], table[:].indirect(entries[:]))
             return picked
 
-        def round_weight(name, raws, copy):
-            grouped = sbuf(name + "_bf16", [P, PACK * S], BF16)
-            view = grouped[:].rearrange("p (t m j) -> p m j t", t=PACK, j=PACK)
-            step = P // len(raws)
-            for h, raw in enumerate(raws):
-                copy(view[:, h * step : (h + 1) * step], raw[:].rearrange("p j (m t) -> p m j t", t=PACK))
-            return grouped
+        def round_weight(name, halves, copy):
+            rounded = sbuf(name + "_bf16", [P, PACK * S], BF16)
+            view = rounded[:].rearrange("p (t m j) -> p m j t", t=PACK, j=PACK)
+            m_half = HALF // PACK
+            for h, raw in enumerate(halves):
+                copy(view[:, h * m_half : (h + 1) * m_half], raw[:].rearrange("p j (m t) -> p m j t", t=PACK))
+            return rounded
 
-        def quantize(name, grouped, width):
+        def quantize(name, rounded, width):
             codes = sbuf(name + "_codes", [P, width], U32)
             scales = sbuf(name + "_scales", [P, width], U8)
-            nc.vector.quantize_mx(out=codes[:].bitcast(FP8X4), scales=scales[:], in_=grouped)
+            nc.vector.quantize_mx(out=codes[:].bitcast(FP8X4), scales=scales[:], in_=rounded)
             return codes, scales
 
         def product(acc, stationary, m0, moving, n0, n):
@@ -94,21 +102,23 @@ def tile_picked_ybeamsl_rate_p_kernel(
                 stop=True,
             )
 
-        xs_table = scale_table("xs_table", x_scales)
-        es_table = scale_table("es_table", e_scales)
+        xs_table = cleared_scale_table("xs_table", x_scales)
+        es_table = cleared_scale_table("es_table", e_scales)
+        u2 = load_factor("u2", unit2)
+        u1 = load_factor("u1", unit)
+        identity = sbuf("identity", [P, P], F32)
+        make_identity(nc, identity[:])
         offs_l = load_list("offs_l", offs)
-        w2_raw = [load_weight("w2", w2, 0)]
+        w2_raw = [load_weight_half("w2", w2, 0)]
         load_scales(xs_table, x_scales)
-        w2_raw.append(load_weight("w2", w2, 1))
+        w2_raw.append(load_weight_half("w2", w2, 1))
+        xw_table = load_words("xw_table", x_words)
         txb_l = load_list("txb_l", txb)
         load_scales(es_table, e_scales)
-        xw_table = load_words("xw_table", x_words)
         ew_table = load_words("ew_table", e_words)
-        w3_raw = [load_weight("w3", w3, h) for h in range(2)]
-        u2 = load_factor("u2", unit2)
+        w3_raw = [load_weight_half("w3", w3, h) for h in range(2)]
         pol_l = load_list("pol_l", pol)
-        w1_raw = [load_weight("w1", w1, h) for h in range(2)]
-        u1 = load_factor("u1", unit)
+        w1_raw = [load_weight_half("w1", w1, h) for h in range(2)]
         noi_sb = sbuf("noi_sb", [P, noi.shape[1]], F32)
         nc.sync.dma_start(noi_sb[:], noi)
         adj_l = load_list("adj_l", adj)
@@ -124,24 +134,29 @@ def tile_picked_ybeamsl_rate_p_kernel(
         for t in range(PACK):
             acc = bank([P, S])
             product(acc[:], w2q, P * t, xq, 0, S)
-            th = sbuf("tanh%d" % t, [P, S], F32)
-            nc.scalar.activation(th[:], acc[:], ACT.Tanh)
-            tanh_im.append(th)
+            tanh_t = sbuf("tanh%d" % t, [P, S], F32)
+            nc.scalar.activation(tanh_t[:], acc[:], ACT.Tanh)
+            tanh_im.append(tanh_t)
 
         ew = gather("ew", ew_table, txb_l, U32)
         eq = (ew, es)
 
-        mod = []
+        partner = []
+        list_half = HALF // GROUP
         for h in range(2):
-            picked = sbuf("mod%d" % h, [P, PACK, HALF], F32)
+            partner_h = sbuf("partner%d" % h, [P, PACK, HALF], F32)
             for t in range(PACK):
                 nc.scalar.activation(
-                    picked[:, t, :], tanh_im[t][:].indirect(pol_l[:, 16 * h : 16 * (h + 1)]), ACT.Copy, bias=0.4
+                    partner_h[:, t, :],
+                    tanh_im[t][:].indirect(pol_l[:, list_half * h : list_half * (h + 1)]),
+                    ACT.Copy,
+                    bias=0.4,
                 )
-            mod.append(picked)
+            partner.append(partner_h)
 
         w3q = quantize("w3", round_weight("w3", w3_raw, nc.vector.tensor_copy)[:], S)
         w1q = quantize("w1", round_weight("w1", w1_raw, nc.vector.tensor_copy)[:], S)
+
         hid2_bf = sbuf("hid2_bf16", [P, S, PACK], BF16)
         for b in range(S // P):
             acc = bank([P, PACK, P])
@@ -155,59 +170,77 @@ def tile_picked_ybeamsl_rate_p_kernel(
             )
         hid2q = quantize("hid2", hid2_bf[:].rearrange("p n t -> p (n t)"), S)
 
-        floor = sbuf("floor", [P, S], F32)
-        nc.scalar.activation(floor[:], noi_sb[:].indirect(txb_l[:]), ACT.Copy, bias=0.4, scale=2.0)
+        noise = sbuf("noise", [P, S], F32)
+        nc.scalar.activation(noise[:], noi_sb[:].indirect(txb_l[:]), ACT.Copy, bias=0.4, scale=2.0)
 
         re = {}
         for h in range(2):
             for pair in range(PACK // 2):
                 acc = bank([P, 2, HALF])
-                for i in range(2):
-                    t = 2 * pair + i
-                    product(acc[:, i, :], w1q, P * t, xq, HALF * h, HALF)
-                    re[h, t] = acc[:, i, :]
+                for side in range(2):
+                    t = 2 * pair + side
+                    product(acc[:, side, :], w1q, P * t, xq, HALF * h, HALF)
+                    re[h, t] = acc[:, side, :]
 
         hidq = []
-        for h in range(2):
-            planes = sbuf("hid_planes%d" % h, [P, PACK, HALF], BF16)
+        for h, interleave in enumerate((nc.scalar.copy, nc.vector.tensor_copy)):
+            hid_rows = sbuf("hid_rows%d" % h, [P, PACK, HALF], BF16)
             for t in range(PACK):
                 nc.vector.scalar_tensor_tensor(
-                    planes[:, t, :],
+                    hid_rows[:, t, :],
                     re[h, t],
                     u1[:, t : t + 1],
-                    mod[h][:, t, :],
+                    partner[h][:, t, :],
                     ALU.mult,
                     ALU.mult,
                 )
             hid_bf = sbuf("hid_bf16_%d" % h, [P, HALF, PACK], BF16)
-            (nc.scalar.copy, nc.vector.tensor_copy)[h](
-                hid_bf[:].rearrange("p (c i) t -> p c t i", i=4),
-                planes[:].rearrange("p t (c i) -> p c t i", i=4),
+            interleave(
+                hid_bf[:].rearrange("p (c w) t -> p c t w", w=LINE),
+                hid_rows[:].rearrange("p t (c w) -> p c t w", w=LINE),
             )
             hidq.append(quantize("hid%d" % h, hid_bf[:].rearrange("p n t -> p (n t)"), HALF))
 
-        windows = []
+        powers = []
+        tiles_in_half = HALF // P
         for a in range(S // P):
             acc = bank([P, S])
-            product(acc[:], hidq[a // 2], P * (a % 2), hid2q, 0, S)
-            window = sbuf("power%d" % a, [P, S + 32], F32)
-            nc.scalar.activation(window[:, :S], acc[:], ACT.Square)
-            windows.append(window)
+            product(acc[:], hidq[a // tiles_in_half], P * (a % tiles_in_half), hid2q, 0, S)
+            power = sbuf("power%d" % a, [P, S + SPARE], F32)
+            nc.scalar.activation(power[:, :S], acc[:], ACT.Square)
+            powers.append(power)
 
-        for a, window in enumerate(windows):
+        for a, power in enumerate(powers):
             den = sbuf("den%d" % a, [P, S], F32)
-            if a == 1:
-                leak = sbuf("leak", [P, S], F32)
-                nc.scalar.activation(leak[:], window[:].indirect(adj_l[:]), ACT.Copy)
-                nc.vector.tensor_tensor(den[:], leak[:], floor[:], ALU.add)
-            else:
-                nc.vector.tensor_tensor(den[:], window[:].indirect(adj_l[:]), floor[:], ALU.add)
-            num = sbuf("num%d" % a, [P, S], F32)
-            nc.vector.scalar_tensor_tensor(num[:], window[:, :S], 2.0, den[:], ALU.mult, ALU.add)
+            nc.vector.tensor_tensor(den[:], power[:].indirect(adj_l[:]), noise[:], ALU.add)
             ln_den = sbuf("ln_den%d" % a, [P, S], F32)
-            nc.scalar.activation(ln_den[:], den[:], ACT.Ln)
             ln_num = sbuf("ln_num%d" % a, [P, S], F32)
-            nc.scalar.activation(ln_num[:], num[:], ACT.Ln)
+            if a < TURNED_TILES:
+                num = bank([P, S])
+                for b in range(S // P):
+                    cols = slice(P * b, P * (b + 1))
+                    terms = (power[:, cols], power[:, cols], den[:, cols])
+                    for place, term in enumerate(terms):
+                        nc.tensor.matmul(
+                            num[:, cols],
+                            term,
+                            identity[:],
+                            start=place == 0,
+                            stop=place == len(terms) - 1,
+                            is_transpose=True,
+                        )
+                nc.scalar.activation(ln_den[:], den[:], ACT.Ln)
+                nc.scalar.activation(ln_num[:], num[:], ACT.Ln)
+                ln_num_upright = bank([P, S])
+                for b in range(S // P):
+                    cols = slice(P * b, P * (b + 1))
+                    nc.tensor.transpose(ln_num_upright[:, cols], ln_num[:, cols], identity[:])
+            else:
+                num = sbuf("num%d" % a, [P, S], F32)
+                nc.vector.scalar_tensor_tensor(num[:], power[:, :S], 2.0, den[:], ALU.mult, ALU.add)
+                nc.scalar.activation(ln_den[:], den[:], ACT.Ln)
+                nc.scalar.activation(ln_num[:], num[:], ACT.Ln)
+                ln_num_upright = ln_num
             rate = sbuf("rate%d" % a, [P, S], F32)
-            nc.vector.tensor_tensor(rate[:], ln_num[:], ln_den[:], ALU.subtract)
+            nc.vector.tensor_tensor(rate[:], ln_num_upright[:], ln_den[:], ALU.subtract)
             nc.sync.dma_start(out[P * a : P * (a + 1), :], rate[:])

from contextlib import ExitStack

import concourse.mybir as mybir
from concourse.masks import make_identity

F32 = mybir.dt.float32
BF16 = mybir.dt.bfloat16
I32 = mybir.dt.int32
U32 = mybir.dt.uint32
U16 = mybir.dt.uint16
U8 = mybir.dt.uint8
FP8X4 = mybir.dt.float8_e4m3fn_x4
ALU = mybir.AluOpType
ACT = mybir.ActivationFunctionType

P = 128
PACK = 4
S = 512
HALF = S // 2
GROUP = 16
QUADRANT = 32
LINE = 4
BANKS = 8
SPARE = 32
TURNED_TILES = 2
FLOPS = 4 * 2 * S * S * S


def tile_picked_ybeamsl_rate_p_kernel(
    tc, x_words, x_scales, w1, w2, e_words, e_scales, w3, unit, unit2, noi, offs, txb, pol, adj, out
):
    nc = tc.nc
    with ExitStack() as ctx:
        keep = ctx.enter_context(tc.tile_pool(name="keep", bufs=1))
        psum = ctx.enter_context(tc.psum_pool(name="psum", bufs=BANKS))

        def sbuf(name, shape, dtype):
            return keep.tile(shape, dtype, name=name, align_bytes=64)

        def bank(shape):
            return psum.tile(shape, F32, name="bank")

        def load_list(name, src):
            entries = sbuf(name, [P, S // GROUP], U16)
            nc.sync.dma_start(entries[:], src)
            return entries

        def load_words(name, src):
            table = sbuf(name, [P, src.shape[2]], U32)
            nc.sync.dma_start(table[:].bitcast(I32), src[0].rearrange("p n j -> p (n j)").bitcast(I32))
            return table

        def cleared_scale_table(name, src):
            table = sbuf(name, [P, src.shape[2]], U8)
            nc.vector.memset(table[:].bitcast(I32), 0)
            return table

        def load_scales(table, src):
            for q in range(P // QUADRANT):
                nc.sync.dma_start(
                    table[QUADRANT * q : QUADRANT * q + 4, :].bitcast(I32),
                    src[0, 4 * q : 4 * q + 4, :].bitcast(I32),
                )

        def load_weight_half(name, src, h):
            raw = sbuf("%s_raw%d" % (name, h), [P, PACK, HALF], F32)
            nc.sync.dma_start(raw[:], src[:, h * HALF : (h + 1) * HALF].rearrange("(p j) c -> p j c", j=PACK))
            return raw

        def load_factor(name, src):
            factor = sbuf(name, [P, PACK], F32)
            nc.gpsimd.dma_start(factor[:], src.rearrange("(p t) o -> p (t o)", t=PACK))
            return factor

        def gather(name, table, entries, dtype):
            picked = sbuf(name, [P, S], dtype)
            nc.vector.tensor_copy(picked[:], table[:].indirect(entries[:]))
            return picked

        def round_weight(name, halves, copy):
            rounded = sbuf(name + "_bf16", [P, PACK * S], BF16)
            view = rounded[:].rearrange("p (t m j) -> p m j t", t=PACK, j=PACK)
            m_half = HALF // PACK
            for h, raw in enumerate(halves):
                copy(view[:, h * m_half : (h + 1) * m_half], raw[:].rearrange("p j (m t) -> p m j t", t=PACK))
            return rounded

        def quantize(name, rounded, width):
            codes = sbuf(name + "_codes", [P, width], U32)
            scales = sbuf(name + "_scales", [P, width], U8)
            nc.vector.quantize_mx(out=codes[:].bitcast(FP8X4), scales=scales[:], in_=rounded)
            return codes, scales

        def product(acc, stationary, m0, moving, n0, n):
            nc.tensor.matmul_mx(
                out=acc,
                lhsT=stationary[0][:, m0 : m0 + P].bitcast(FP8X4),
                lhsT_scale=stationary[1][:, m0 : m0 + P],
                rhs=moving[0][:, n0 : n0 + n].bitcast(FP8X4),
                rhs_scale=moving[1][:, n0 : n0 + n],
                start=True,
                stop=True,
            )

        xs_table = cleared_scale_table("xs_table", x_scales)
        es_table = cleared_scale_table("es_table", e_scales)
        u2 = load_factor("u2", unit2)
        u1 = load_factor("u1", unit)
        identity = sbuf("identity", [P, P], F32)
        make_identity(nc, identity[:])
        offs_l = load_list("offs_l", offs)
        w2_raw = [load_weight_half("w2", w2, 0)]
        load_scales(xs_table, x_scales)
        w2_raw.append(load_weight_half("w2", w2, 1))
        xw_table = load_words("xw_table", x_words)
        txb_l = load_list("txb_l", txb)
        load_scales(es_table, e_scales)
        ew_table = load_words("ew_table", e_words)
        w3_raw = [load_weight_half("w3", w3, h) for h in range(2)]
        pol_l = load_list("pol_l", pol)
        w1_raw = [load_weight_half("w1", w1, h) for h in range(2)]
        noi_sb = sbuf("noi_sb", [P, noi.shape[1]], F32)
        nc.sync.dma_start(noi_sb[:], noi)
        adj_l = load_list("adj_l", adj)

        xs = gather("xs", xs_table, offs_l, U8)
        w2_bf = round_weight("w2", w2_raw, nc.scalar.copy)
        es = gather("es", es_table, txb_l, U8)
        w2q = quantize("w2", w2_bf[:], S)
        xw = gather("xw", xw_table, offs_l, U32)
        xq = (xw, xs)

        tanh_im = []
        for t in range(PACK):
            acc = bank([P, S])
            product(acc[:], w2q, P * t, xq, 0, S)
            tanh_t = sbuf("tanh%d" % t, [P, S], F32)
            nc.scalar.activation(tanh_t[:], acc[:], ACT.Tanh)
            tanh_im.append(tanh_t)

        ew = gather("ew", ew_table, txb_l, U32)
        eq = (ew, es)

        partner = []
        list_half = HALF // GROUP
        for h in range(2):
            partner_h = sbuf("partner%d" % h, [P, PACK, HALF], F32)
            for t in range(PACK):
                nc.scalar.activation(
                    partner_h[:, t, :],
                    tanh_im[t][:].indirect(pol_l[:, list_half * h : list_half * (h + 1)]),
                    ACT.Copy,
                    bias=0.4,
                )
            partner.append(partner_h)

        w3q = quantize("w3", round_weight("w3", w3_raw, nc.vector.tensor_copy)[:], S)
        w1q = quantize("w1", round_weight("w1", w1_raw, nc.vector.tensor_copy)[:], S)

        hid2_bf = sbuf("hid2_bf16", [P, S, PACK], BF16)
        for b in range(S // P):
            acc = bank([P, PACK, P])
            for t in range(PACK):
                product(acc[:, t, :], w3q, P * t, eq, P * b, P)
            nc.vector.tensor_tensor(
                hid2_bf[:, P * b : P * (b + 1), :],
                acc[:].rearrange("p t n -> p n t"),
                u2[:].unsqueeze(1).to_broadcast([P, P, PACK]),
                ALU.mult,
            )
        hid2q = quantize("hid2", hid2_bf[:].rearrange("p n t -> p (n t)"), S)

        noise = sbuf("noise", [P, S], F32)
        nc.scalar.activation(noise[:], noi_sb[:].indirect(txb_l[:]), ACT.Copy, bias=0.4, scale=2.0)

        re = {}
        for h in range(2):
            for pair in range(PACK // 2):
                acc = bank([P, 2, HALF])
                for side in range(2):
                    t = 2 * pair + side
                    product(acc[:, side, :], w1q, P * t, xq, HALF * h, HALF)
                    re[h, t] = acc[:, side, :]

        hidq = []
        for h, interleave in enumerate((nc.scalar.copy, nc.vector.tensor_copy)):
            hid_rows = sbuf("hid_rows%d" % h, [P, PACK, HALF], BF16)
            for t in range(PACK):
                nc.vector.scalar_tensor_tensor(
                    hid_rows[:, t, :],
                    re[h, t],
                    u1[:, t : t + 1],
                    partner[h][:, t, :],
                    ALU.mult,
                    ALU.mult,
                )
            hid_bf = sbuf("hid_bf16_%d" % h, [P, HALF, PACK], BF16)
            interleave(
                hid_bf[:].rearrange("p (c w) t -> p c t w", w=LINE),
                hid_rows[:].rearrange("p t (c w) -> p c t w", w=LINE),
            )
            hidq.append(quantize("hid%d" % h, hid_bf[:].rearrange("p n t -> p (n t)"), HALF))

        powers = []
        tiles_in_half = HALF // P
        for a in range(S // P):
            acc = bank([P, S])
            product(acc[:], hidq[a // tiles_in_half], P * (a % tiles_in_half), hid2q, 0, S)
            power = sbuf("power%d" % a, [P, S + SPARE], F32)
            nc.scalar.activation(power[:, :S], acc[:], ACT.Square)
            powers.append(power)

        for a, power in enumerate(powers):
            den = sbuf("den%d" % a, [P, S], F32)
            nc.vector.tensor_tensor(den[:], power[:].indirect(adj_l[:]), noise[:], ALU.add)
            ln_den = sbuf("ln_den%d" % a, [P, S], F32)
            ln_num = sbuf("ln_num%d" % a, [P, S], F32)
            if a < TURNED_TILES:
                num = bank([P, S])
                for b in range(S // P):
                    cols = slice(P * b, P * (b + 1))
                    terms = (power[:, cols], power[:, cols], den[:, cols])
                    for place, term in enumerate(terms):
                        nc.tensor.matmul(
                            num[:, cols],
                            term,
                            identity[:],
                            start=place == 0,
                            stop=place == len(terms) - 1,
                            is_transpose=True,
                        )
                nc.scalar.activation(ln_den[:], den[:], ACT.Ln)
                nc.scalar.activation(ln_num[:], num[:], ACT.Ln)
                ln_num_upright = bank([P, S])
                for b in range(S // P):
                    cols = slice(P * b, P * (b + 1))
                    nc.tensor.transpose(ln_num_upright[:, cols], ln_num[:, cols], identity[:])
            else:
                num = sbuf("num%d" % a, [P, S], F32)
                nc.vector.scalar_tensor_tensor(num[:], power[:, :S], 2.0, den[:], ALU.mult, ALU.add)
                nc.scalar.activation(ln_den[:], den[:], ACT.Ln)
                nc.scalar.activation(ln_num[:], num[:], ACT.Ln)
                ln_num_upright = ln_num
            rate = sbuf("rate%d" % a, [P, S], F32)
            nc.vector.tensor_tensor(rate[:], ln_num_upright[:], ln_den[:], ALU.subtract)
            nc.sync.dma_start(out[P * a : P * (a + 1), :], rate[:])
